import numpy as np
import ml_dtypes


def mxq(x, axis, fmt="e4m3"):
    dtype, down = {"e4m3": (ml_dtypes.float8_e4m3fn, 7), "e5m2": (ml_dtypes.float8_e5m2, 14)}[fmt]
    v = np.moveaxis(np.asarray(x, np.float32).astype(ml_dtypes.bfloat16).astype(np.float64), axis, -1)
    blocks = v.reshape(v.shape[:-1] + (-1, 32))
    amax = np.abs(blocks).max(-1, keepdims=True)
    byte = np.maximum(np.where(amax > 0, np.frexp(amax)[1] - 1 + 127, 0) - down, 1)
    scale = np.exp2(byte - 127.0)
    codes = (blocks / scale).astype(np.float32).astype(dtype).astype(np.float64)
    return np.moveaxis((codes * scale).reshape(v.shape), -1, axis)


WIDE = False


def mx_kscale(k):
    if not WIDE:
        return np.ones(k)
    levels = np.array([10, -10, 5, -5, 0])
    if k % 512:
        return np.exp2(np.random.permutation(np.resize(levels, k // 32))).repeat(32)
    a = np.empty((k // 512, 16))
    for p in range(k // 512):
        a[p, :8] = np.random.permutation(np.resize(levels, 8))
        for g in range(8):
            far = levels[np.abs(levels - a[p, g]) >= 10]
            a[p, g + 8] = far[np.random.randint(len(far))]
    return np.exp2(a.ravel()).repeat(32)


def f64(x):
    return np.asarray(x).astype(np.float64)


def striped(idx):
    return np.tile(np.asarray(idx).reshape(-1, 16).T, (8, 1)).astype(np.uint16)


def unstriped(offs):
    return offs[:16].T.reshape(-1).astype(np.int64)


E2M1 = np.array([0.0, 0.5, 1.0, 1.5, 2.0, 3.0, 4.0, 6.0, -0.0, -0.5, -1.0, -1.5, -2.0, -3.0, -4.0, -6.0])


def pack_weight(w, fmt):
    k, n = w.shape
    w = f64(np.asarray(w, np.float32).astype(ml_dtypes.bfloat16)).reshape(k // 32, 32, n)
    amax = np.abs(w).max(1)
    if fmt == "e4m3":
        byte = np.frexp(amax)[1] - 1 + 127 - 7
    else:
        mant, ex = np.frexp(amax / 6.0)
        byte = np.where(mant > 0.5, ex, ex - 1) + 127
    byte = np.clip(np.where(amax > 0, byte, 1), 1, 254)
    scaled = (w * np.exp2(127.0 - byte)[:, None, :]).reshape(k, n).astype(np.float32)
    by_word = np.ascontiguousarray(scaled.reshape(k // 512, 128, 4, n).transpose(0, 1, 3, 2))
    if fmt == "e4m3":
        words = by_word.astype(ml_dtypes.float8_e4m3fn).view(np.uint8)
    else:
        c = by_word.astype(ml_dtypes.float4_e2m1fn).view(np.uint8) & 0xF
        words = (c[..., 0::2] | (c[..., 1::2] << 4)).reshape(k // 512, 128, 2 * n)
    return np.ascontiguousarray(words), np.ascontiguousarray(byte.astype(np.uint8).reshape(k // 512, 16, n))


def unpack_weight(words, scales, fmt):
    g, _, n = scales.shape
    words = np.ascontiguousarray(words).reshape(g, 128, n, -1)
    if fmt == "e4m3":
        vals = words.view(ml_dtypes.float8_e4m3fn).astype(np.float64)
    else:
        nib = np.empty((g, 128, n, 4), np.uint8)
        nib[..., 0::2] = words & 0xF
        nib[..., 1::2] = words >> 4
        vals = E2M1[nib]
    vals = vals * np.repeat(np.exp2(scales.astype(np.float64) - 127.0), 8, axis=1)[..., None]
    return vals.transpose(0, 1, 3, 2).reshape(g * 512, n)


D, K, R, T, I, Q, G = 512, 512, 512, 2048, 512, 128, 64


def setup_inputs():
    n = np.random.standard_normal
    idx = np.random.permutation(T)[:I]
    fd = mx_kscale(D)
    fk = mx_kscale(K)
    fi = mx_kscale(I)
    keysp = pack_weight(n((D, T)) / fd[:, None], "e4m3")
    tabp = pack_weight(n((K, T)) / fk[:, None], "e4m3")
    return {
        "query": (n((D, Q)) * 0.6 / np.sqrt(D) * fd[:, None]).astype(np.float32),
        "keys_words": keysp[0],
        "keys_scales": keysp[1],
        "sharp": (np.random.uniform(1.0, 3.0, (Q, 1))).astype(np.float32),
        "tab_words": tabp[0],
        "tab_scales": tabp[1],
        "w1": (n((K, R)) * 1 / np.sqrt(K) * fk[:, None]).astype(np.float32),
        "temper": (np.random.uniform(0.4, 1.0, (R, 1))).astype(np.float32),
        "os": (np.random.uniform(4.0, 16.0, (1, I)) * fi).astype(np.float32),
        "vs": (np.random.uniform(0.5, 2.0, (1, I)) / fi).astype(np.float32),
        "offs": striped(idx),
    }


def reference(query, keys_words, keys_scales, sharp, tab_words, tab_scales, w1, temper, os, vs, offs):
    idx = unstriped(offs)
    keysu = unpack_weight(keys_words, keys_scales, "e4m3")
    tabu = unpack_weight(tab_words, tab_scales, "e4m3")
    queryq = mxq(f64(query), 0, "e4m3")
    keysidxg = keysu[:, idx]
    a = queryq.T @ keysidxg
    p = np.exp(a)
    s = p.reshape(Q, G, I // G).sum(axis=2)
    ms = a.reshape(Q, G, I // G).mean(axis=2) * f64(sharp)
    pg = np.exp(ms - np.max(ms, axis=1, keepdims=True))
    z = np.sum(pg, axis=1, keepdims=True)
    sh = pg / z / s
    rr = np.repeat(sh, I // G, axis=1)
    w = p * rr
    w1q = mxq(f64(w1), 0, "e4m3")
    tabidxg = tabu[:, idx]
    zh = w1q.T @ tabidxg
    ht = np.exp(zh * f64(temper))
    mz = ht.reshape(R, G, I // G).sum(axis=2)
    mzr = np.repeat(mz, I // G, axis=1)
    hv = ht / mzr * 4.0
    wo1 = w * f64(os)
    wt1 = wo1.T
    hw = hv * f64(vs)
    ht1 = hw.T
    wt1q = mxq(wt1, 0, "e4m3")
    ht1q = mxq(ht1, 0, "e4m3")
    o = wt1q.T @ ht1q
    return o

@@ -1,0 +1,237 @@
+from contextlib import ExitStack
+
+import concourse.mybir as mybir
+from concourse.masks import make_identity
+
+F32 = mybir.dt.float32
+BF16 = mybir.dt.bfloat16
+I32 = mybir.dt.int32
+U32 = mybir.dt.uint32
+U16 = mybir.dt.uint16
+U8 = mybir.dt.uint8
+FP8X4 = mybir.dt.float8_e4m3fn_x4
+ALU = mybir.AluOpType
+ACT = mybir.ActivationFunctionType
+AX = mybir.AxisListType
+
+P = 128
+D, K, R, T, I, Q, G = 512, 512, 512, 2048, 512, 128, 64
+FLOPS = 2 * D * Q * I + 2 * K * R * I + 2 * I * Q * R
+
+
+def tile_attend_lrshared_bygroup_kernel(
+    tc, query, keys_words, keys_scales, sharp, tab_words, tab_scales, w1, temper, slot_os, slot_vs, offs, out
+):
+    nc = tc.nc
+    with ExitStack() as ctx:
+        lists = ctx.enter_context(tc.tile_pool(name="lists", bufs=1))
+        sb = ctx.enter_context(tc.tile_pool(name="sb", bufs=1))
+        late = ctx.enter_context(tc.tile_pool(name="late", bufs=1))
+        ps_z = ctx.enter_context(tc.psum_pool(name="ps_z", bufs=2))
+        ps_t = ctx.enter_context(tc.psum_pool(name="ps_t", bufs=2))
+        ps_s = ctx.enter_context(tc.psum_pool(name="ps_s", bufs=2))
+        ps_a = ctx.enter_context(tc.psum_pool(name="ps_a", bufs=1))
+
+        on_keys = {"key_pool": 0, "inv_t1": 0, "dup0": 512, "ev0": 2048}
+
+        def tile(shape, dtype, name):
+            if name in on_keys:
+                return late.tile(shape, dtype, name=name, align_bytes=64, offset=on_keys[name])
+            return sb.tile(shape, dtype, name=name, align_bytes=64)
+
+        offsets = lists.tile([P, I // 16], U16, name="offsets")
+        nc.sync.dma_start(offsets[:], offs)
+
+        def load_words(words, name):
+            pool_words = tile([P, T], I32, name)
+            nc.sync.dma_start(pool_words[:], words[0].rearrange("p n t -> p (n t)").bitcast(I32))
+            return pool_words
+
+        def load_w1(h):
+            raw = tile([P, 4, 256], F32, "w_raw%d" % h)
+            nc.sync.dma_start(raw[:], w1.rearrange("(p j) r -> p j r", j=4)[:, :, 256 * h : 256 * (h + 1)])
+            return raw
+
+        tab_plane = tile([P, T], U8, "tab_plane")
+        for quad in range(4):
+            nc.sync.dma_start(
+                tab_plane[32 * quad : 32 * quad + 32, :].bitcast(I32),
+                tab_scales[0, 4 * quad : 4 * quad + 4, :].bitcast(I32).unsqueeze(0).to_broadcast([8, 4, T // 4]),
+            )
+        key_plane = tile([P, T], U8, "key_plane")
+        nc.gpsimd.memset(key_plane[:].bitcast(I32), 0)
+        tab_pool = load_words(tab_words, "tab_pool")
+        w_raw = [load_w1(0)]
+        temper_t = tile([P, 4], F32, "temper_t")
+        with nc.allow_non_contiguous_dma(reason="one value a partition"):
+            nc.sync.dma_start(temper_t[:], temper.rearrange("(t p) o -> p (t o)", p=P))
+        w_raw.append(load_w1(1))
+        for quad in range(4):
+            nc.sync.dma_start(
+                key_plane[32 * quad : 32 * quad + 4, :].bitcast(I32),
+                keys_scales[0, 4 * quad : 4 * quad + 4, :].bitcast(I32),
+            )
+        q_raw = tile([P, 4, Q], F32, "q_raw")
+        nc.sync.dma_start(q_raw[:], query.rearrange("(p j) q -> p j q", j=4))
+        key_pool = load_words(keys_words, "key_pool")
+        vs_t = tile([P, 4], F32, "vs_t")
+        nc.sync.dma_start(vs_t[:], slot_vs.rearrange("o (p t) -> p (o t)", t=4))
+        sharp_t = tile([P, 1], F32, "sharp_t")
+        nc.sync.dma_start(sharp_t[:], sharp)
+        os_t = tile([P, 4], F32, "os_t")
+        nc.sync.dma_start(os_t[:], slot_os.rearrange("o (p t) -> p (o t)", t=4))
+        ident = tile([P, P], F32, "ident")
+        make_identity(nc, ident[:])
+
+        def gather(window, dtype, name):
+            got = tile([P, I], dtype, name)
+            nc.vector.tensor_copy(got[:], window.indirect(offsets[:]))
+            return got
+
+        def cast_interleave(raw, name, on_scalar):
+            grouped = tile([P, P, 4], BF16, name)
+            dst = grouped[:].rearrange("p (c i) t -> p c t i", i=4)
+            src = raw.rearrange("p t (c i) -> p c t i", i=4)
+            if on_scalar:
+                nc.scalar.activation(dst, src, ACT.Copy)
+            else:
+                nc.vector.tensor_copy(dst, src)
+            return grouped
+
+        def quantise(grouped, width, name):
+            codes = tile([P, width], U32, name + "_codes")
+            plane = tile([P, width], U8, name + "_plane")
+            nc.vector.quantize_mx(codes[:].bitcast(FP8X4), plane[:], grouped.rearrange("p w t -> p (w t)"))
+            return codes, plane
+
+        def product(dst, lhs, rhs):
+            nc.tensor.matmul_mx(
+                dst, lhsT=lhs[0].bitcast(FP8X4), lhsT_scale=lhs[1], rhs=rhs[0].bitcast(FP8X4), rhs_scale=rhs[1],
+                start=True, stop=True,
+            )
+
+        tab_s = gather(tab_plane[:], U8, "tab_s")
+        tab_w = gather(tab_pool[:].bitcast(U32), U32, "tab_w")
+
+        def layer(h, scalar_casts):
+            e = tile([P, 4, 2, P], F32, "e_pair%d" % h)
+            for u in range(2):
+                rt = 2 * h + u
+                grouped = cast_interleave(w_raw[h][:, :, P * u : P * (u + 1)], "w_bf%d" % rt, u in scalar_casts)
+                codes, plane = quantise(grouped[:], P, "w_q%d" % rt)
+                z = ps_z.tile([P, I], F32, name="z", tag="z")
+                product(z[:], (codes[:], plane[:]), (tab_w[:], tab_s[:]))
+                nc.scalar.activation(
+                    e[:, :, u, :], z[:].rearrange("r (p t) -> r t p", t=4), ACT.Exp, scale=temper_t[:, rt : rt + 1]
+                )
+            return e
+
+        def normalisers(h, e):
+            small = ps_s.tile([P, 512], F32, name="small", tag="small")
+            flat = e[:].rearrange("r t u p -> r t (u p)")
+            for j in range(8):
+                t, half = j % 4, j // 4
+                nc.tensor.matmul(
+                    small[:, 0:P], flat[:, t, half : 2 * P : 2], ident[:], start=(j == 0), stop=(j == 7), is_transpose=True
+                )
+            inv_t = tile([P, P], F32, "inv_t%d" % h)
+            nc.vector.reciprocal(inv_t[:], small[:, 0:P])
+            nc.tensor.transpose(small[:, P : 2 * P], inv_t[:], ident[:])
+            dup = tile([P, P, 2], F32, "dup%d" % h)
+            nc.scalar.activation(
+                dup[:], small[:, P : 2 * P].unsqueeze(2).to_broadcast([P, P, 2]), ACT.Copy, scale=4.0
+            )
+            dup_flat = dup[:].rearrange("r x e -> r (x e)")
+            for u in range(2):
+                nc.tensor.transpose(small[:, P * (2 + u) : P * (3 + u)], dup_flat[:, P * u : P * (u + 1)], ident[:])
+            return small
+
+        def turn_and_scale(h, e):
+            ev = tile([P, 64, 4, 4], F32, "ev%d" % h)
+            for b in range(2):
+                bank = ps_t.tile([P, 2, 2, P], F32, name="turned", tag="turned")
+                for tt in range(2):
+                    for u in range(2):
+                        nc.tensor.transpose(bank[:, tt, u, :], e[:, 2 * b + tt, u, :], ident[:])
+                for tt in range(2):
+                    t = 2 * b + tt
+                    nc.scalar.activation(
+                        ev[:, :, t, :], bank[:, tt].rearrange("p u (c i) -> p (u c) i", i=4), ACT.Copy,
+                        scale=vs_t[:, t : t + 1],
+                    )
+            return ev
+
+        def finish(dst, values, factor):
+            nc.vector.tensor_tensor(
+                dst.rearrange("p (c i) t -> p c t i", i=4),
+                values,
+                factor.rearrange("p (c i) -> p c i", i=4).unsqueeze(2).to_broadcast([P, 32, 4, 4]),
+                ALU.mult,
+            )
+
+        e0 = layer(0, (1,))
+        e1 = layer(1, ())
+        key_s = gather(key_plane[:], U8, "key_s")
+        q_bf = cast_interleave(q_raw[:], "q_bf", True)
+        q_codes, q_plane = quantise(q_bf[:], Q, "q_q")
+        key_w = gather(key_pool[:].bitcast(U32), U32, "key_w")
+        a = ps_a.tile([P, I], F32, name="a", tag="a")
+        product(a[:], (q_codes[:], q_plane[:]), (key_w[:], key_s[:]))
+        pe = tile([P, 4, P], F32, "pe")
+        nc.scalar.activation(pe[:], a[:].rearrange("q (p t) -> q t p", t=4), ACT.Exp)
+
+        g0 = normalisers(0, e0)
+        g1 = normalisers(1, e1)
+        neg_sharp = tile([P, 1], F32, "neg_sharp")
+        nc.scalar.activation(neg_sharp[:], sharp_t[:], ACT.Copy, scale=-0.125)
+        sum_a = tile([P, G], F32, "sum_a")
+        nc.vector.tensor_reduce(sum_a[:], a[:].rearrange("q (g j) -> q g j", j=8), AX.X, ALU.add)
+        neg_ms = tile([P, G], F32, "neg_ms")
+        neg_max = tile([P, 1], F32, "neg_max")
+        nc.vector.tensor_scalar(neg_ms[:], sum_a[:], neg_sharp[:], None, ALU.mult, ALU.min, accum_out=neg_max[:])
+        pg = tile([P, G], F32, "pg")
+        zsum = tile([P, 1], F32, "zsum")
+        nc.scalar.activation(pg[:], neg_ms[:], ACT.Exp, bias=neg_max[:], scale=-1.0, accum_out=zsum[:])
+        sum_p = tile([P, G], F32, "sum_p")
+        nc.vector.tensor_reduce(sum_p[:], pe[:].rearrange("q t (g e) -> q g t e", e=2), AX.XY, ALU.add)
+        inv_s = tile([P, G], F32, "inv_s")
+        nc.vector.reciprocal(inv_s[:], sum_p[:])
+        inv_z = tile([P, 1], F32, "inv_z")
+        nc.vector.reciprocal(inv_z[:], zsum[:])
+        sh = tile([P, G, 2], F32, "sh")
+        nc.vector.scalar_tensor_tensor(
+            sh[:], pg[:].unsqueeze(2).to_broadcast([P, G, 2]), inv_z[:], inv_s[:].unsqueeze(2).to_broadcast([P, G, 2]),
+            ALU.mult, ALU.mult,
+        )
+        sh_t = ps_a.tile([P, 512], F32, name="a", tag="a")
+        nc.tensor.transpose(sh_t[:, 0:P], sh[:].rearrange("q g e -> q (g e)"), ident[:])
+
+        ev0 = turn_and_scale(0, e0)
+
+        p_bank = ps_z.tile([P, 4, P], F32, name="z", tag="z")
+        for t in range(4):
+            nc.tensor.transpose(p_bank[:, t, :], pe[:, t, :], ident[:])
+        po = tile([P, 32, 4, 4], F32, "po")
+        for t in range(4):
+            nc.scalar.activation(
+                po[:, :, t, :], p_bank[:, t].rearrange("p (c i) -> p c i", i=4), ACT.Copy, scale=os_t[:, t : t + 1]
+            )
+        ev1 = turn_and_scale(1, e1)
+
+        wt_bf = tile([P, Q, 4], BF16, "wt_bf")
+        finish(wt_bf[:], po[:], sh_t[:, 0:P])
+        wt_q = quantise(wt_bf[:], Q, "wt_q")
+
+        ht_q = []
+        for h, (ev, g) in enumerate(((ev0, g0), (ev1, g1))):
+            ht_bf = tile([P, 2 * P, 4], BF16, "ht_bf%d" % h)
+            for u in range(2):
+                finish(ht_bf[:, P * u : P * (u + 1), :], ev[:, 32 * u : 32 * (u + 1)], g[:, P * (2 + u) : P * (3 + u)])
+            ht_q.append(quantise(ht_bf[:], 2 * P, "ht_q%d" % h))
+
+        for h in range(2):
+            o = ps_z.tile([P, I], F32, name="z", tag="z")
+            product(o[:, 0:256], (wt_q[0][:], wt_q[1][:]), (ht_q[h][0][:], ht_q[h][1][:]))
+            res = tile([P, 256], F32, "res%d" % h)
+            nc.scalar.copy(res[:], o[:, 0:256])
+            nc.sync.dma_start(out[:, 256 * h : 256 * (h + 1)], res[:])

@@ -32,7 +32,7 @@ def tile_attend_lrshared_bygroup_kernel(
         ps_s = ctx.enter_context(tc.psum_pool(name="ps_s", bufs=2))
         ps_a = ctx.enter_context(tc.psum_pool(name="ps_a", bufs=1))
 
-        on_keys = {"key_pool": 0, "inv_t1": 0, "dup0": 512, "ev0": 2048}
+        on_keys = {"key_pool": 0, "inv_t1": 0, "dup0": 512, "ev0": 2048, "key_plane": 8192, "inv_t0": 8192, "key_w": 9216}
 
         def tile(shape, dtype, name):
             if name in on_keys:
@@ -58,16 +58,19 @@ def tile_attend_lrshared_bygroup_kernel(
                 tab_plane[32 * quad : 32 * quad + 32, :].bitcast(I32),
                 tab_scales[0, 4 * quad : 4 * quad + 4, :].bitcast(I32).unsqueeze(0).to_broadcast([8, 4, T // 4]),
             )
+        rows = tile([P, P], F32, "rows")
+        nc.gpsimd.memset(rows[:], 0.0)
+        ident = tile([P, P], F32, "ident")
+        nc.gpsimd.memset(ident[:], 0.0)
         key_plane = tile([P, T], U8, "key_plane")
         nc.gpsimd.memset(key_plane[:].bitcast(I32), 0)
+        make_identity(nc, ident[:], nomemset=True)
         tab_pool = load_words(tab_words, "tab_pool")
         w_raw = [load_w1(0)]
-        temper_t = tile([P, 4], F32, "temper_t")
-        with nc.allow_non_contiguous_dma(reason="one value a partition"):
-            nc.sync.dma_start(temper_t[:], temper.rearrange("(t p) o -> p (t o)", p=P))
+        nc.sync.dma_start(rows[0:4, :], temper.rearrange("(t p) o -> t (p o)", p=P))
         w_raw.append(load_w1(1))
         for quad in range(4):
-            nc.sync.dma_start(
+            nc.gpsimd.dma_start(
                 key_plane[32 * quad : 32 * quad + 4, :].bitcast(I32),
                 keys_scales[0, 4 * quad : 4 * quad + 4, :].bitcast(I32),
             )
@@ -80,8 +83,10 @@ def tile_attend_lrshared_bygroup_kernel(
         nc.sync.dma_start(sharp_t[:], sharp)
         os_t = tile([P, 4], F32, "os_t")
         nc.sync.dma_start(os_t[:], slot_os.rearrange("o (p t) -> p (o t)", t=4))
-        ident = tile([P, P], F32, "ident")
-        make_identity(nc, ident[:])
+        rows_t = ps_a.tile([P, 512], F32, name="a", tag="a")
+        nc.tensor.transpose(rows_t[:, 0:P], rows[:], ident[:])
+        temper_t = tile([P, 4], F32, "temper_t")
+        nc.scalar.activation(temper_t[:], rows_t[:, 0:4], ACT.Copy)
 
         def gather(window, dtype, name):
             got = tile([P, I], dtype, name)

@@ -27,12 +27,13 @@ def tile_attend_lrshared_bygroup_kernel(
         lists = ctx.enter_context(tc.tile_pool(name="lists", bufs=1))
         sb = ctx.enter_context(tc.tile_pool(name="sb", bufs=1))
         late = ctx.enter_context(tc.tile_pool(name="late", bufs=1))
-        ps_z = ctx.enter_context(tc.psum_pool(name="ps_z", bufs=2))
+        ps_z = ctx.enter_context(tc.psum_pool(name="ps_z", bufs=3))
         ps_t = ctx.enter_context(tc.psum_pool(name="ps_t", bufs=2))
         ps_s = ctx.enter_context(tc.psum_pool(name="ps_s", bufs=2))
         ps_a = ctx.enter_context(tc.psum_pool(name="ps_a", bufs=1))
 
-        on_keys = {"key_pool": 0, "inv_t1": 0, "dup0": 512, "ev0": 2048, "key_plane": 8192, "inv_t0": 8192, "key_w": 9216}
+        on_keys = {"key_pool": 0, "inv_t1": 0, "dup0": 512, "ev0": 2048, "key_plane": 8192, "inv_t0": 8192, "w_q2_codes": 8704, "key_w": 9216,
+                   "w_raw1": 12288, "e_pair0": 12288}
 
         def tile(shape, dtype, name):
             if name in on_keys:
@@ -59,12 +60,11 @@ def tile_attend_lrshared_bygroup_kernel(
                 tab_scales[0, 4 * quad : 4 * quad + 4, :].bitcast(I32).unsqueeze(0).to_broadcast([8, 4, T // 4]),
             )
         rows = tile([P, P], F32, "rows")
-        nc.gpsimd.memset(rows[:], 0.0)
+        nc.vector.memset(rows[:], 0.0)
         ident = tile([P, P], F32, "ident")
-        nc.gpsimd.memset(ident[:], 0.0)
+        nc.vector.memset(ident[:], 0.0)
         key_plane = tile([P, T], U8, "key_plane")
         nc.gpsimd.memset(key_plane[:].bitcast(I32), 0)
-        make_identity(nc, ident[:], nomemset=True)
         tab_pool = load_words(tab_words, "tab_pool")
         w_raw = [load_w1(0)]
         nc.sync.dma_start(rows[0:4, :], temper.rearrange("(t p) o -> t (p o)", p=P))
@@ -74,6 +74,7 @@ def tile_attend_lrshared_bygroup_kernel(
                 key_plane[32 * quad : 32 * quad + 4, :].bitcast(I32),
                 keys_scales[0, 4 * quad : 4 * quad + 4, :].bitcast(I32),
             )
+        make_identity(nc, ident[:], nomemset=True)
         q_raw = tile([P, 4, Q], F32, "q_raw")
         nc.sync.dma_start(q_raw[:], query.rearrange("(p j) q -> p j q", j=4))
         key_pool = load_words(keys_words, "key_pool")
@@ -151,6 +152,20 @@ def tile_attend_lrshared_bygroup_kernel(
                 nc.tensor.transpose(small[:, P * (2 + u) : P * (3 + u)], dup_flat[:, P * u : P * (u + 1)], ident[:])
             return small
 
+        def normalisers_by_vector(h, e):
+            sums = tile([P, 2, G], F32, "sums%d" % h)
+            for u in range(2):
+                nc.vector.tensor_reduce(sums[:, u, :], e[:, :, u, :].rearrange("r t (g e) -> r g t e", e=2), AX.XY, ALU.add)
+            inv = tile([P, P], F32, "inv_t%d" % h)
+            nc.vector.reciprocal(inv[:], sums[:].rearrange("r u g -> r (u g)"))
+            dup = tile([P, P, 2], F32, "dup%d" % h)
+            nc.scalar.activation(dup[:], inv[:].unsqueeze(2).to_broadcast([P, P, 2]), ACT.Copy, scale=4.0)
+            small = ps_s.tile([P, 512], F32, name="small", tag="small")
+            dup_flat = dup[:].rearrange("r x e -> r (x e)")
+            for u in range(2):
+                nc.tensor.transpose(small[:, P * (2 + u) : P * (3 + u)], dup_flat[:, P * u : P * (u + 1)], ident[:])
+            return small
+
         def turn_and_scale(h, e):
             ev = tile([P, 64, 4, 4], F32, "ev%d" % h)
             for b in range(2):
@@ -175,7 +190,7 @@ def tile_attend_lrshared_bygroup_kernel(
             )
 
         e0 = layer(0, (1,))
-        e1 = layer(1, ())
+        e1 = layer(1, (0, 1))
         key_s = gather(key_plane[:], U8, "key_s")
         q_bf = cast_interleave(q_raw[:], "q_bf", True)
         q_codes, q_plane = quantise(q_bf[:], Q, "q_q")
@@ -185,7 +200,7 @@ def tile_attend_lrshared_bygroup_kernel(
         pe = tile([P, 4, P], F32, "pe")
         nc.scalar.activation(pe[:], a[:].rearrange("q (p t) -> q t p", t=4), ACT.Exp)
 
-        g0 = normalisers(0, e0)
+        g0 = normalisers_by_vector(0, e0)
         g1 = normalisers(1, e1)
         neg_sharp = tile([P, 1], F32, "neg_sharp")
         nc.scalar.activation(neg_sharp[:], sharp_t[:], ACT.Copy, scale=-0.125)
@@ -227,16 +242,21 @@ def tile_attend_lrshared_bygroup_kernel(
         finish(wt_bf[:], po[:], sh_t[:, 0:P])
         wt_q = quantise(wt_bf[:], Q, "wt_q")
 
-        ht_q = []
-        for h, (ev, g) in enumerate(((ev0, g0), (ev1, g1))):
-            ht_bf = tile([P, 2 * P, 4], BF16, "ht_bf%d" % h)
-            for u in range(2):
-                finish(ht_bf[:, P * u : P * (u + 1), :], ev[:, 32 * u : 32 * (u + 1)], g[:, P * (2 + u) : P * (3 + u)])
-            ht_q.append(quantise(ht_bf[:], 2 * P, "ht_q%d" % h))
+        def emit(first, width, ht_bf, bank):
+            codes, plane = quantise(ht_bf, width, "ht_q%d" % first)
+            product(bank[:, 0:width], (wt_q[0][:], wt_q[1][:]), (codes[:], plane[:]))
+            res = tile([P, width], F32, "res%d" % first)
+            nc.scalar.copy(res[:], bank[:, 0:width])
+            nc.sync.dma_start(out[:, first : first + width], res[:])
 
-        for h in range(2):
-            o = ps_z.tile([P, I], F32, name="z", tag="z")
-            product(o[:, 0:256], (wt_q[0][:], wt_q[1][:]), (ht_q[h][0][:], ht_q[h][1][:]))
-            res = tile([P, 256], F32, "res%d" % h)
-            nc.scalar.copy(res[:], o[:, 0:256])
-            nc.sync.dma_start(out[:, 256 * h : 256 * (h + 1)], res[:])
+        ht_bf0 = tile([P, 2 * P, 4], BF16, "ht_bf0")
+        for u in range(2):
+            finish(ht_bf0[:, P * u : P * (u + 1), :], ev0[:, 32 * u : 32 * (u + 1)], g0[:, P * (2 + u) : P * (3 + u)])
+        emit(0, 2 * P, ht_bf0[:], ps_z.tile([P, I], F32, name="z", tag="z"))
+        last = []
+        for u in range(2):
+            ht_bf = tile([P, P, 4], BF16, "ht_bf%d" % (2 + u))
+            finish(ht_bf[:], ev1[:, 32 * u : 32 * (u + 1)], g1[:, P * (2 + u) : P * (3 + u)])
+            last.append(ht_bf)
+        for u in range(2):
+            emit(P * (2 + u), P, last[u][:], ps_z.tile([P, I], F32, name="z", tag="z"))

@@ -27,13 +27,12 @@ def tile_attend_lrshared_bygroup_kernel(
         lists = ctx.enter_context(tc.tile_pool(name="lists", bufs=1))
         sb = ctx.enter_context(tc.tile_pool(name="sb", bufs=1))
         late = ctx.enter_context(tc.tile_pool(name="late", bufs=1))
-        ps_z = ctx.enter_context(tc.psum_pool(name="ps_z", bufs=3))
-        ps_t = ctx.enter_context(tc.psum_pool(name="ps_t", bufs=2))
-        ps_s = ctx.enter_context(tc.psum_pool(name="ps_s", bufs=2))
-        ps_a = ctx.enter_context(tc.psum_pool(name="ps_a", bufs=1))
+        psum = ctx.enter_context(tc.psum_pool(name="psum", bufs=1))
 
-        on_keys = {"key_pool": 0, "inv_t1": 0, "dup0": 512, "ev0": 2048, "key_plane": 8192, "inv_t0": 8192, "w_q2_codes": 8704, "key_w": 9216,
-                   "w_raw1": 12288, "e_pair0": 12288}
+        def bank(number, name, shape=(P, 512)):
+            return psum.tile(list(shape), F32, name=name, offset=2048 * number)
+
+        on_keys = {"key_pool": 0, "inv_t0": 0, "temper_last": 512}
 
         def tile(shape, dtype, name):
             if name in on_keys:
@@ -60,23 +59,23 @@ def tile_attend_lrshared_bygroup_kernel(
                 tab_scales[0, 4 * quad : 4 * quad + 4, :].bitcast(I32).unsqueeze(0).to_broadcast([8, 4, T // 4]),
             )
         rows = tile([P, P], F32, "rows")
-        nc.vector.memset(rows[:], 0.0)
+        nc.gpsimd.memset(rows[:], 0.0)
         ident = tile([P, P], F32, "ident")
-        nc.vector.memset(ident[:], 0.0)
+        nc.gpsimd.memset(ident[:], 0.0)
         key_plane = tile([P, T], U8, "key_plane")
         nc.gpsimd.memset(key_plane[:].bitcast(I32), 0)
+        make_identity(nc, ident[:], nomemset=True)
         tab_pool = load_words(tab_words, "tab_pool")
+        q_raw = tile([P, 4, Q], F32, "q_raw")
+        nc.sync.dma_start(q_raw[:], query.rearrange("(p j) q -> p j q", j=4))
         w_raw = [load_w1(0)]
         nc.sync.dma_start(rows[0:4, :], temper.rearrange("(t p) o -> t (p o)", p=P))
         w_raw.append(load_w1(1))
         for quad in range(4):
-            nc.gpsimd.dma_start(
+            nc.sync.dma_start(
                 key_plane[32 * quad : 32 * quad + 4, :].bitcast(I32),
                 keys_scales[0, 4 * quad : 4 * quad + 4, :].bitcast(I32),
             )
-        make_identity(nc, ident[:], nomemset=True)
-        q_raw = tile([P, 4, Q], F32, "q_raw")
-        nc.sync.dma_start(q_raw[:], query.rearrange("(p j) q -> p j q", j=4))
         key_pool = load_words(keys_words, "key_pool")
         vs_t = tile([P, 4], F32, "vs_t")
         nc.sync.dma_start(vs_t[:], slot_vs.rearrange("o (p t) -> p (o t)", t=4))
@@ -84,10 +83,13 @@ def tile_attend_lrshared_bygroup_kernel(
         nc.sync.dma_start(sharp_t[:], sharp)
         os_t = tile([P, 4], F32, "os_t")
         nc.sync.dma_start(os_t[:], slot_os.rearrange("o (p t) -> p (o t)", t=4))
-        rows_t = ps_a.tile([P, 512], F32, name="a", tag="a")
+        rows_t = bank(2, "rows_t")
         nc.tensor.transpose(rows_t[:, 0:P], rows[:], ident[:])
-        temper_t = tile([P, 4], F32, "temper_t")
-        nc.scalar.activation(temper_t[:], rows_t[:, 0:4], ACT.Copy)
+        temper_t = tile([P, 3], F32, "temper_t")
+        nc.scalar.activation(temper_t[:], rows_t[:, 0:3], ACT.Copy)
+        temper_last = tile([P, 1], F32, "temper_last")
+        nc.scalar.activation(temper_last[:], rows_t[:, 3:4], ACT.Copy)
+        tempers = [temper_t[:, 0:1], temper_t[:, 1:2], temper_t[:, 2:3], temper_last[:]]
 
         def gather(window, dtype, name):
             got = tile([P, I], dtype, name)
@@ -125,15 +127,15 @@ def tile_attend_lrshared_bygroup_kernel(
                 rt = 2 * h + u
                 grouped = cast_interleave(w_raw[h][:, :, P * u : P * (u + 1)], "w_bf%d" % rt, u in scalar_casts)
                 codes, plane = quantise(grouped[:], P, "w_q%d" % rt)
-                z = ps_z.tile([P, I], F32, name="z", tag="z")
+                z = bank((0, 1, 7, 3)[rt], "z%d" % rt)
                 product(z[:], (codes[:], plane[:]), (tab_w[:], tab_s[:]))
                 nc.scalar.activation(
-                    e[:, :, u, :], z[:].rearrange("r (p t) -> r t p", t=4), ACT.Exp, scale=temper_t[:, rt : rt + 1]
+                    e[:, :, u, :], z[:].rearrange("r (p t) -> r t p", t=4), ACT.Exp, scale=tempers[rt]
                 )
             return e
 
         def normalisers(h, e):
-            small = ps_s.tile([P, 512], F32, name="small", tag="small")
+            small = bank(5 + h, "small%d" % h)
             flat = e[:].rearrange("r t u p -> r t (u p)")
             for j in range(8):
                 t, half = j % 4, j // 4
@@ -152,31 +154,17 @@ def tile_attend_lrshared_bygroup_kernel(
                 nc.tensor.transpose(small[:, P * (2 + u) : P * (3 + u)], dup_flat[:, P * u : P * (u + 1)], ident[:])
             return small
 
-        def normalisers_by_vector(h, e):
-            sums = tile([P, 2, G], F32, "sums%d" % h)
-            for u in range(2):
-                nc.vector.tensor_reduce(sums[:, u, :], e[:, :, u, :].rearrange("r t (g e) -> r g t e", e=2), AX.XY, ALU.add)
-            inv = tile([P, P], F32, "inv_t%d" % h)
-            nc.vector.reciprocal(inv[:], sums[:].rearrange("r u g -> r (u g)"))
-            dup = tile([P, P, 2], F32, "dup%d" % h)
-            nc.scalar.activation(dup[:], inv[:].unsqueeze(2).to_broadcast([P, P, 2]), ACT.Copy, scale=4.0)
-            small = ps_s.tile([P, 512], F32, name="small", tag="small")
-            dup_flat = dup[:].rearrange("r x e -> r (x e)")
-            for u in range(2):
-                nc.tensor.transpose(small[:, P * (2 + u) : P * (3 + u)], dup_flat[:, P * u : P * (u + 1)], ident[:])
-            return small
-
         def turn_and_scale(h, e):
             ev = tile([P, 64, 4, 4], F32, "ev%d" % h)
             for b in range(2):
-                bank = ps_t.tile([P, 2, 2, P], F32, name="turned", tag="turned")
+                turned = bank(((2, 3), (0, 7))[h][b], "turned%d%d" % (h, b), (P, 2, 2, P))
                 for tt in range(2):
                     for u in range(2):
-                        nc.tensor.transpose(bank[:, tt, u, :], e[:, 2 * b + tt, u, :], ident[:])
+                        nc.tensor.transpose(turned[:, tt, u, :], e[:, 2 * b + tt, u, :], ident[:])
                 for tt in range(2):
                     t = 2 * b + tt
                     nc.scalar.activation(
-                        ev[:, :, t, :], bank[:, tt].rearrange("p u (c i) -> p (u c) i", i=4), ACT.Copy,
+                        ev[:, :, t, :], turned[:, tt].rearrange("p u (c i) -> p (u c) i", i=4), ACT.Copy,
                         scale=vs_t[:, t : t + 1],
                     )
             return ev
@@ -185,23 +173,21 @@ def tile_attend_lrshared_bygroup_kernel(
             nc.vector.tensor_tensor(
                 dst.rearrange("p (c i) t -> p c t i", i=4),
                 values,
-                factor.rearrange("p (c i) -> p c i", i=4).unsqueeze(2).to_broadcast([P, 32, 4, 4]),
+                factor.rearrange("p (c i) -> p c i", i=4).unsqueeze(2).to_broadcast(list(values.shape)),
                 ALU.mult,
             )
 
         e0 = layer(0, (1,))
-        e1 = layer(1, (0, 1))
         key_s = gather(key_plane[:], U8, "key_s")
         q_bf = cast_interleave(q_raw[:], "q_bf", True)
         q_codes, q_plane = quantise(q_bf[:], Q, "q_q")
+        e1 = layer(1, ())
         key_w = gather(key_pool[:].bitcast(U32), U32, "key_w")
-        a = ps_a.tile([P, I], F32, name="a", tag="a")
+        a = bank(4, "a")
         product(a[:], (q_codes[:], q_plane[:]), (key_w[:], key_s[:]))
         pe = tile([P, 4, P], F32, "pe")
         nc.scalar.activation(pe[:], a[:].rearrange("q (p t) -> q t p", t=4), ACT.Exp)
 
-        g0 = normalisers_by_vector(0, e0)
-        g1 = normalisers(1, e1)
         neg_sharp = tile([P, 1], F32, "neg_sharp")
         nc.scalar.activation(neg_sharp[:], sharp_t[:], ACT.Copy, scale=-0.125)
         sum_a = tile([P, G], F32, "sum_a")
@@ -223,12 +209,14 @@ def tile_attend_lrshared_bygroup_kernel(
             sh[:], pg[:].unsqueeze(2).to_broadcast([P, G, 2]), inv_z[:], inv_s[:].unsqueeze(2).to_broadcast([P, G, 2]),
             ALU.mult, ALU.mult,
         )
-        sh_t = ps_a.tile([P, 512], F32, name="a", tag="a")
+        sh_t = bank(4, "sh_t")
         nc.tensor.transpose(sh_t[:, 0:P], sh[:].rearrange("q g e -> q (g e)"), ident[:])
 
+        g0 = normalisers(0, e0)
+        g1 = normalisers(1, e1)
         ev0 = turn_and_scale(0, e0)
 
-        p_bank = ps_z.tile([P, 4, P], F32, name="z", tag="z")
+        p_bank = bank(1, "p_bank", (P, 4, P))
         for t in range(4):
             nc.tensor.transpose(p_bank[:, t, :], pe[:, t, :], ident[:])
         po = tile([P, 32, 4, 4], F32, "po")
@@ -242,21 +230,20 @@ def tile_attend_lrshared_bygroup_kernel(
         finish(wt_bf[:], po[:], sh_t[:, 0:P])
         wt_q = quantise(wt_bf[:], Q, "wt_q")
 
-        def emit(first, width, ht_bf, bank):
+        def emit(first, width, ht_bf, acc):
             codes, plane = quantise(ht_bf, width, "ht_q%d" % first)
-            product(bank[:, 0:width], (wt_q[0][:], wt_q[1][:]), (codes[:], plane[:]))
+            product(acc[:, 0:width], (wt_q[0][:], wt_q[1][:]), (codes[:], plane[:]))
             res = tile([P, width], F32, "res%d" % first)
-            nc.scalar.copy(res[:], bank[:, 0:width])
+            nc.scalar.copy(res[:], acc[:, 0:width])
             nc.sync.dma_start(out[:, first : first + width], res[:])
 
         ht_bf0 = tile([P, 2 * P, 4], BF16, "ht_bf0")
-        for u in range(2):
-            finish(ht_bf0[:, P * u : P * (u + 1), :], ev0[:, 32 * u : 32 * (u + 1)], g0[:, P * (2 + u) : P * (3 + u)])
-        emit(0, 2 * P, ht_bf0[:], ps_z.tile([P, I], F32, name="z", tag="z"))
+        finish(ht_bf0[:], ev0[:], g0[:, 2 * P : 4 * P])
+        emit(0, 2 * P, ht_bf0[:], bank(2, "acc0"))
         last = []
         for u in range(2):
             ht_bf = tile([P, P, 4], BF16, "ht_bf%d" % (2 + u))
             finish(ht_bf[:], ev1[:, 32 * u : 32 * (u + 1)], g1[:, P * (2 + u) : P * (3 + u)])
             last.append(ht_bf)
         for u in range(2):
-            emit(P * (2 + u), P, last[u][:], ps_z.tile([P, I], F32, name="z", tag="z"))
+            emit(P * (2 + u), P, last[u][:], bank((3, 1)[u], "acc%d" % (2 + u)))

from contextlib import ExitStack

import concourse.mybir as mybir
from concourse.masks import make_identity

F32 = mybir.dt.float32
BF16 = mybir.dt.bfloat16
I32 = mybir.dt.int32
U32 = mybir.dt.uint32
U16 = mybir.dt.uint16
U8 = mybir.dt.uint8
FP8X4 = mybir.dt.float8_e4m3fn_x4
ALU = mybir.AluOpType
ACT = mybir.ActivationFunctionType
AX = mybir.AxisListType

P = 128
D, K, R, T, I, Q, G = 512, 512, 512, 2048, 512, 128, 64
FLOPS = 2 * D * Q * I + 2 * K * R * I + 2 * I * Q * R


def tile_attend_lrshared_bygroup_kernel(
    tc, query, keys_words, keys_scales, sharp, tab_words, tab_scales, w1, temper, slot_os, slot_vs, offs, out
):
    nc = tc.nc
    with ExitStack() as ctx:
        lists = ctx.enter_context(tc.tile_pool(name="lists", bufs=1))
        sb = ctx.enter_context(tc.tile_pool(name="sb", bufs=1))
        late = ctx.enter_context(tc.tile_pool(name="late", bufs=1))
        psum = ctx.enter_context(tc.psum_pool(name="psum", bufs=1))

        def bank(number, name, shape=(P, 512)):
            return psum.tile(list(shape), F32, name=name, offset=2048 * number)

        on_keys = {"key_pool": 0, "inv_t0": 0, "temper_last": 512}

        def tile(shape, dtype, name):
            if name in on_keys:
                return late.tile(shape, dtype, name=name, align_bytes=64, offset=on_keys[name])
            return sb.tile(shape, dtype, name=name, align_bytes=64)

        offsets = lists.tile([P, I // 16], U16, name="offsets")
        nc.sync.dma_start(offsets[:], offs)

        def load_words(words, name):
            pool_words = tile([P, T], I32, name)
            nc.sync.dma_start(pool_words[:], words[0].rearrange("p n t -> p (n t)").bitcast(I32))
            return pool_words

        def load_w1(h):
            raw = tile([P, 4, 256], F32, "w_raw%d" % h)
            nc.sync.dma_start(raw[:], w1.rearrange("(p j) r -> p j r", j=4)[:, :, 256 * h : 256 * (h + 1)])
            return raw

        tab_plane = tile([P, T], U8, "tab_plane")
        for quad in range(4):
            nc.sync.dma_start(
                tab_plane[32 * quad : 32 * quad + 32, :].bitcast(I32),
                tab_scales[0, 4 * quad : 4 * quad + 4, :].bitcast(I32).unsqueeze(0).to_broadcast([8, 4, T // 4]),
            )
        rows = tile([P, P], F32, "rows")
        nc.gpsimd.memset(rows[:], 0.0)
        ident = tile([P, P], F32, "ident")
        nc.gpsimd.memset(ident[:], 0.0)
        key_plane = tile([P, T], U8, "key_plane")
        nc.gpsimd.memset(key_plane[:].bitcast(I32), 0)
        make_identity(nc, ident[:], nomemset=True)
        tab_pool = load_words(tab_words, "tab_pool")
        q_raw = tile([P, 4, Q], F32, "q_raw")
        nc.sync.dma_start(q_raw[:], query.rearrange("(p j) q -> p j q", j=4))
        w_raw = [load_w1(0)]
        nc.sync.dma_start(rows[0:4, :], temper.rearrange("(t p) o -> t (p o)", p=P))
        w_raw.append(load_w1(1))
        for quad in range(4):
            nc.sync.dma_start(
                key_plane[32 * quad : 32 * quad + 4, :].bitcast(I32),
                keys_scales[0, 4 * quad : 4 * quad + 4, :].bitcast(I32),
            )
        key_pool = load_words(keys_words, "key_pool")
        vs_t = tile([P, 4], F32, "vs_t")
        nc.sync.dma_start(vs_t[:], slot_vs.rearrange("o (p t) -> p (o t)", t=4))
        sharp_t = tile([P, 1], F32, "sharp_t")
        nc.sync.dma_start(sharp_t[:], sharp)
        os_t = tile([P, 4], F32, "os_t")
        nc.sync.dma_start(os_t[:], slot_os.rearrange("o (p t) -> p (o t)", t=4))
        rows_t = bank(2, "rows_t")
        nc.tensor.transpose(rows_t[:, 0:P], rows[:], ident[:])
        temper_t = tile([P, 3], F32, "temper_t")
        nc.scalar.activation(temper_t[:], rows_t[:, 0:3], ACT.Copy)
        temper_last = tile([P, 1], F32, "temper_last")
        nc.scalar.activation(temper_last[:], rows_t[:, 3:4], ACT.Copy)
        tempers = [temper_t[:, 0:1], temper_t[:, 1:2], temper_t[:, 2:3], temper_last[:]]

        def gather(window, dtype, name):
            got = tile([P, I], dtype, name)
            nc.vector.tensor_copy(got[:], window.indirect(offsets[:]))
            return got

        def cast_interleave(raw, name, on_scalar):
            grouped = tile([P, P, 4], BF16, name)
            dst = grouped[:].rearrange("p (c i) t -> p c t i", i=4)
            src = raw.rearrange("p t (c i) -> p c t i", i=4)
            if on_scalar:
                nc.scalar.activation(dst, src, ACT.Copy)
            else:
                nc.vector.tensor_copy(dst, src)
            return grouped

        def quantise(grouped, width, name):
            codes = tile([P, width], U32, name + "_codes")
            plane = tile([P, width], U8, name + "_plane")
            nc.vector.quantize_mx(codes[:].bitcast(FP8X4), plane[:], grouped.rearrange("p w t -> p (w t)"))
            return codes, plane

        def product(dst, lhs, rhs):
            nc.tensor.matmul_mx(
                dst, lhsT=lhs[0].bitcast(FP8X4), lhsT_scale=lhs[1], rhs=rhs[0].bitcast(FP8X4), rhs_scale=rhs[1],
                start=True, stop=True,
            )

        tab_s = gather(tab_plane[:], U8, "tab_s")
        tab_w = gather(tab_pool[:].bitcast(U32), U32, "tab_w")

        def layer(h, scalar_casts):
            e = tile([P, 4, 2, P], F32, "e_pair%d" % h)
            for u in range(2):
                rt = 2 * h + u
                grouped = cast_interleave(w_raw[h][:, :, P * u : P * (u + 1)], "w_bf%d" % rt, u in scalar_casts)
                codes, plane = quantise(grouped[:], P, "w_q%d" % rt)
                z = bank((0, 1, 7, 3)[rt], "z%d" % rt)
                product(z[:], (codes[:], plane[:]), (tab_w[:], tab_s[:]))
                nc.scalar.activation(
                    e[:, :, u, :], z[:].rearrange("r (p t) -> r t p", t=4), ACT.Exp, scale=tempers[rt]
                )
            return e

        def normalisers(h, e):
            small = bank(5 + h, "small%d" % h)
            flat = e[:].rearrange("r t u p -> r t (u p)")
            for j in range(8):
                t, half = j % 4, j // 4
                nc.tensor.matmul(
                    small[:, 0:P], flat[:, t, half : 2 * P : 2], ident[:], start=(j == 0), stop=(j == 7), is_transpose=True
                )
            inv_t = tile([P, P], F32, "inv_t%d" % h)
            nc.vector.reciprocal(inv_t[:], small[:, 0:P])
            nc.tensor.transpose(small[:, P : 2 * P], inv_t[:], ident[:])
            dup = tile([P, P, 2], F32, "dup%d" % h)
            nc.scalar.activation(
                dup[:], small[:, P : 2 * P].unsqueeze(2).to_broadcast([P, P, 2]), ACT.Copy, scale=4.0
            )
            dup_flat = dup[:].rearrange("r x e -> r (x e)")
            for u in range(2):
                nc.tensor.transpose(small[:, P * (2 + u) : P * (3 + u)], dup_flat[:, P * u : P * (u + 1)], ident[:])
            return small

        def turn_and_scale(h, e):
            ev = tile([P, 64, 4, 4], F32, "ev%d" % h)
            for b in range(2):
                turned = bank(((2, 3), (0, 7))[h][b], "turned%d%d" % (h, b), (P, 2, 2, P))
                for tt in range(2):
                    for u in range(2):
                        nc.tensor.transpose(turned[:, tt, u, :], e[:, 2 * b + tt, u, :], ident[:])
                for tt in range(2):
                    t = 2 * b + tt
                    nc.scalar.activation(
                        ev[:, :, t, :], turned[:, tt].rearrange("p u (c i) -> p (u c) i", i=4), ACT.Copy,
                        scale=vs_t[:, t : t + 1],
                    )
            return ev

        def finish(dst, values, factor):
            nc.vector.tensor_tensor(
                dst.rearrange("p (c i) t -> p c t i", i=4),
                values,
                factor.rearrange("p (c i) -> p c i", i=4).unsqueeze(2).to_broadcast(list(values.shape)),
                ALU.mult,
            )

        e0 = layer(0, (1,))
        key_s = gather(key_plane[:], U8, "key_s")
        q_bf = cast_interleave(q_raw[:], "q_bf", True)
        q_codes, q_plane = quantise(q_bf[:], Q, "q_q")
        e1 = layer(1, ())
        key_w = gather(key_pool[:].bitcast(U32), U32, "key_w")
        a = bank(4, "a")
        product(a[:], (q_codes[:], q_plane[:]), (key_w[:], key_s[:]))
        pe = tile([P, 4, P], F32, "pe")
        nc.scalar.activation(pe[:], a[:].rearrange("q (p t) -> q t p", t=4), ACT.Exp)

        neg_sharp = tile([P, 1], F32, "neg_sharp")
        nc.scalar.activation(neg_sharp[:], sharp_t[:], ACT.Copy, scale=-0.125)
        sum_a = tile([P, G], F32, "sum_a")
        nc.vector.tensor_reduce(sum_a[:], a[:].rearrange("q (g j) -> q g j", j=8), AX.X, ALU.add)
        neg_ms = tile([P, G], F32, "neg_ms")
        neg_max = tile([P, 1], F32, "neg_max")
        nc.vector.tensor_scalar(neg_ms[:], sum_a[:], neg_sharp[:], None, ALU.mult, ALU.min, accum_out=neg_max[:])
        pg = tile([P, G], F32, "pg")
        zsum = tile([P, 1], F32, "zsum")
        nc.scalar.activation(pg[:], neg_ms[:], ACT.Exp, bias=neg_max[:], scale=-1.0, accum_out=zsum[:])
        sum_p = tile([P, G], F32, "sum_p")
        nc.vector.tensor_reduce(sum_p[:], pe[:].rearrange("q t (g e) -> q g t e", e=2), AX.XY, ALU.add)
        inv_s = tile([P, G], F32, "inv_s")
        nc.vector.reciprocal(inv_s[:], sum_p[:])
        inv_z = tile([P, 1], F32, "inv_z")
        nc.vector.reciprocal(inv_z[:], zsum[:])
        sh = tile([P, G, 2], F32, "sh")
        nc.vector.scalar_tensor_tensor(
            sh[:], pg[:].unsqueeze(2).to_broadcast([P, G, 2]), inv_z[:], inv_s[:].unsqueeze(2).to_broadcast([P, G, 2]),
            ALU.mult, ALU.mult,
        )
        sh_t = bank(4, "sh_t")
        nc.tensor.transpose(sh_t[:, 0:P], sh[:].rearrange("q g e -> q (g e)"), ident[:])

        g0 = normalisers(0, e0)
        g1 = normalisers(1, e1)
        ev0 = turn_and_scale(0, e0)

        p_bank = bank(1, "p_bank", (P, 4, P))
        for t in range(4):
            nc.tensor.transpose(p_bank[:, t, :], pe[:, t, :], ident[:])
        po = tile([P, 32, 4, 4], F32, "po")
        for t in range(4):
            nc.scalar.activation(
                po[:, :, t, :], p_bank[:, t].rearrange("p (c i) -> p c i", i=4), ACT.Copy, scale=os_t[:, t : t + 1]
            )
        ev1 = turn_and_scale(1, e1)

        wt_bf = tile([P, Q, 4], BF16, "wt_bf")
        finish(wt_bf[:], po[:], sh_t[:, 0:P])
        wt_q = quantise(wt_bf[:], Q, "wt_q")

        def emit(first, width, ht_bf, acc):
            codes, plane = quantise(ht_bf, width, "ht_q%d" % first)
            product(acc[:, 0:width], (wt_q[0][:], wt_q[1][:]), (codes[:], plane[:]))
            res = tile([P, width], F32, "res%d" % first)
            nc.scalar.copy(res[:], acc[:, 0:width])
            nc.sync.dma_start(out[:, first : first + width], res[:])

        ht_bf0 = tile([P, 2 * P, 4], BF16, "ht_bf0")
        finish(ht_bf0[:], ev0[:], g0[:, 2 * P : 4 * P])
        emit(0, 2 * P, ht_bf0[:], bank(2, "acc0"))
        last = []
        for u in range(2):
            ht_bf = tile([P, P, 4], BF16, "ht_bf%d" % (2 + u))
            finish(ht_bf[:], ev1[:, 32 * u : 32 * (u + 1)], g1[:, P * (2 + u) : P * (3 + u)])
            last.append(ht_bf)
        for u in range(2):
            emit(P * (2 + u), P, last[u][:], bank((3, 1)[u], "acc%d" % (2 + u)))
